import numpy as np, ml_dtypes
CORES = [10,34,74,98]
N = 4
TK = 512
def setup_inputs(rng):
    return {"x": rng.standard_normal((N, 128, TK), dtype=np.float32).astype(ml_dtypes.bfloat16), "w1": (rng.standard_normal((N, 128, 128), dtype=np.float32) / 8).astype(ml_dtypes.bfloat16), "w2": (rng.standard_normal((N, 128, 128), dtype=np.float32) / 8).astype(ml_dtypes.bfloat16)}
def setup_inputs_big(rng):
    d = setup_inputs(rng)
    for k in ("x", "w1", "w2"): d[k] = (d[k].astype(np.float32) * 1024.0).astype(d[k].dtype)
    return d
def setup_inputs_small(rng):
    d = setup_inputs(rng)
    for k in ("x", "w1", "w2"): d[k] = (d[k].astype(np.float32) * (1 / 1024.0)).astype(d[k].dtype)
    return d
def setup_inputs_apart(rng):
    d = setup_inputs(rng)
    f = (10.0 ** rng.permutation(np.linspace(-1.5, 1.5, N))).astype(np.float32).reshape(N, 1, 1)
    for k in ("x", "w1", "w2"): d[k] = (d[k].astype(np.float32) * f).astype(d[k].dtype)
    return d
def reference(x, w1, w2):
    X, W1, W2 = x.astype(np.float64), w1.astype(np.float64), w2.astype(np.float64)
    y = np.zeros((N, 128, TK))
    for r in range(N):
        for j in range(N):
            y[r] += W2[j].T @ np.maximum(W1[j].T @ X[r], 0.0)
    return {"y": y.astype(ml_dtypes.bfloat16 if x.dtype != np.float64 else np.float64)}

@@ -1,0 +1,111 @@
+from concourse.mybir import AluOpType
+
+N = 4
+TK = 512
+HALF = TK // 2
+D = 128
+STEPS = (1, 3, 2)
+
+SCRATCH = {
+    "xs": ("sbuf", [128, TK], "bfloat16"),
+    "zero": ("sbuf", [128, HALF], "float32"),
+    "ys0": ("sbuf", [128, HALF], "bfloat16"),
+    "ys1": ("sbuf", [128, HALF], "bfloat16"),
+    "acc0": ("psum", [128, 512], "float32"),
+    "acc1": ("psum", [128, 512], "float32"),
+}
+for _j in range(N):
+    SCRATCH["wp%d" % _j] = ("sbuf", [128, 2 * D], "bfloat16")
+    for _c in range(2):
+        SCRATCH["h%d%d" % (_j, _c)] = ("sbuf", [128, HALF], "bfloat16")
+for _b in range(6):
+    SCRATCH["p%d" % _b] = ("psum", [128, 512], "float32")
+
+SEMAPHORES = ["ldw", "ldx", "zs", "sent", "st0", "st1", "m20", "m21", "cp0", "cp1"]
+SEMAPHORES += ["arr%d" % _j for _j in range(N)]
+SEMAPHORES += ["m1%d%d" % (_k, _c) for _k in range(N) for _c in range(2)]
+SEMAPHORES += ["rl%d%d" % (_k, _c) for _k in range(N) for _c in range(2)]
+
+
+def _bits(mask):
+    n = 0
+    while mask:
+        n += mask & 1
+        mask >>= 1
+    return n
+
+
+def rank_program(g, core, T, topo):
+    r = T.rank_of(core)
+    if r is None:
+        return
+    te, ve, sy, sc = g.tensor, g.vector, g.sync, g.scalar
+    S = T.sem
+    own = T["wp%d" % r]
+
+    sy.dma_start(own[:, 0:D], T.w1[:, :]).then_inc(S.ldw, 16)
+    sc.dma_start(own[:, D:2 * D], T.w2[:, :]).then_inc(S.ldw, 16)
+    sy.dma_start(T.xs[:, 0:HALF], T.x[:, 0:HALF]).then_inc(S.ldx, 16)
+    sc.dma_start(T.xs[:, HALF:TK], T.x[:, HALF:TK]).then_inc(S.ldx, 16)
+    ve.memset(T.zero[:, :], 0.0).then_inc(S.zs, 1)
+
+    g.wait_ge(S.ldw, 32)
+    left = 0
+    for s in STEPS:
+        dst = T.cores[(r + s) % N]
+        assert topo.may_write(core, dst)
+        rid, pid, _ = topo.addr(dst)
+        m = topo.mask(core, dst)
+        g.remote_dma(own[:, :], own[:, :], S["arr%d" % r], S.sent, pid, rid, m)
+        left += _bits(m)
+
+    order = [r] + [(r - s) % N for s in STEPS]
+
+    def mm1(k):
+        w = T["wp%d" % order[k]]
+        for c in range(2):
+            te.matmul(T["p%d" % (2 * (k % 3) + c)][:, 0:HALF], w[:, 0:D], T.xs[:, c * HALF:(c + 1) * HALF],
+                      True, True).then_inc(S["m1%d%d" % (k, c)], 1)
+
+    def mm2(k):
+        w = T["wp%d" % order[k]]
+        for c in range(2):
+            te.wait_ge(S["rl%d%d" % (k, c)], 1)
+            i = te.matmul(T["acc%d" % c][:, 0:HALF], w[:, D:2 * D], T["h%d%d" % (k, c)][:, :], k == 0, k == N - 1)
+            if k == N - 1:
+                i.then_inc(S["m2%d" % c], 1)
+
+    def arrived(k):
+        src = T.cores[order[k]]
+        te.wait_ge(S["arr%d" % order[k]], _bits(topo.mask(src, core)))
+
+    te.wait_ge(S.ldw, 32)
+    te.wait_ge(S.ldx, 32)
+    mm1(0)
+    mm2(0)
+    arrived(1)
+    mm1(1)
+    arrived(2)
+    mm1(2)
+    mm2(1)
+    mm2(2)
+    arrived(3)
+    mm1(3)
+    mm2(3)
+
+    ve.wait_ge(S.zs, 1)
+    for k in range(N):
+        for c in range(2):
+            ve.wait_ge(S["m1%d%d" % (k, c)], 1)
+            ve.tensor_tensor(T["h%d%d" % (k, c)][:, :], T["p%d" % (2 * (k % 3) + c)][:, 0:HALF], T.zero[:, :],
+                             AluOpType.max).then_inc(S["rl%d%d" % (k, c)], 1)
+    for c in range(2):
+        ve.wait_ge(S["m2%d" % c], 1)
+        ve.tensor_copy(T["ys%d" % c][:, :], T["acc%d" % c][:, 0:HALF]).then_inc(S["cp%d" % c], 1)
+
+    for c, q in ((0, sy), (1, sc)):
+        q.wait_ge(S["cp%d" % c], 1)
+        q.dma_start(T.y[:, c * HALF:(c + 1) * HALF], T["ys%d" % c][:, :]).then_inc(S["st%d" % c], 16)
+        q.wait_ge(S["st%d" % c], 16)
+
+    g.wait_ge(S.sent, left)

@@ -5,6 +5,7 @@ TK = 512
 HALF = TK // 2
 D = 128
 STEPS = (1, 3, 2)
+PIECES = ((0, 1), (0, 2), (1, 1), (0, 3), (1, 2), (1, 3))
 
 SCRATCH = {
     "xs": ("sbuf", [128, TK], "bfloat16"),
@@ -21,8 +22,8 @@ for _j in range(N):
 for _b in range(6):
     SCRATCH["p%d" % _b] = ("psum", [128, 512], "float32")
 
-SEMAPHORES = ["ldw", "ldx", "zs", "sent", "st0", "st1", "m20", "m21", "cp0", "cp1"]
-SEMAPHORES += ["arr%d" % _j for _j in range(N)]
+SEMAPHORES = ["ldw1", "ldw2", "ldx", "zs", "sent", "st0", "st1", "m20", "m21", "cp0", "cp1"]
+SEMAPHORES += ["arr%d%d" % (_a, _j) for _a in range(2) for _j in range(N)]
 SEMAPHORES += ["m1%d%d" % (_k, _c) for _k in range(N) for _c in range(2)]
 SEMAPHORES += ["rl%d%d" % (_k, _c) for _k in range(N) for _c in range(2)]
 
@@ -43,20 +44,25 @@ def rank_program(g, core, T, topo):
     S = T.sem
     own = T["wp%d" % r]
 
-    sy.dma_start(own[:, 0:D], T.w1[:, :]).then_inc(S.ldw, 16)
-    sc.dma_start(own[:, D:2 * D], T.w2[:, :]).then_inc(S.ldw, 16)
-    sy.dma_start(T.xs[:, 0:HALF], T.x[:, 0:HALF]).then_inc(S.ldx, 16)
-    sc.dma_start(T.xs[:, HALF:TK], T.x[:, HALF:TK]).then_inc(S.ldx, 16)
+    sy.dma_start(own[0:64, 0:D], T.w1[0:64, :]).then_inc(S.ldw1, 16)
+    sc.dma_start(own[64:128, 0:D], T.w1[64:128, :]).then_inc(S.ldw1, 16)
+    sy.dma_start(own[:, D:2 * D], T.w2[:, :]).then_inc(S.ldw2, 16)
+    sc.dma_start(T.xs[:, :], T.x[:, :]).then_inc(S.ldx, 16)
     ve.memset(T.zero[:, :], 0.0).then_inc(S.zs, 1)
 
-    g.wait_ge(S.ldw, 32)
+    g.wait_ge(S.ldw1, 32)
     left = 0
-    for s in STEPS:
-        dst = T.cores[(r + s) % N]
+    have_w2 = False
+    for a, k in PIECES:
+        if a == 1 and not have_w2:
+            g.wait_ge(S.ldw2, 16)
+            have_w2 = True
+        dst = T.cores[(r + STEPS[k - 1]) % N]
         assert topo.may_write(core, dst)
         rid, pid, _ = topo.addr(dst)
         m = topo.mask(core, dst)
-        g.remote_dma(own[:, :], own[:, :], S["arr%d" % r], S.sent, pid, rid, m)
+        ap = own[:, a * D:(a + 1) * D]
+        g.remote_dma(ap, ap, S["arr%d%d" % (a, r)], S.sent, pid, rid, m)
         left += _bits(m)
 
     order = [r] + [(r - s) % N for s in STEPS]
@@ -75,23 +81,17 @@ def rank_program(g, core, T, topo):
             if k == N - 1:
                 i.then_inc(S["m2%d" % c], 1)
 
-    def arrived(k):
-        src = T.cores[order[k]]
-        te.wait_ge(S["arr%d" % order[k]], _bits(topo.mask(src, core)))
-
-    te.wait_ge(S.ldw, 32)
-    te.wait_ge(S.ldx, 32)
+    te.wait_ge(S.ldw1, 32)
+    te.wait_ge(S.ldx, 16)
     mm1(0)
+    te.wait_ge(S.ldw2, 16)
     mm2(0)
-    arrived(1)
-    mm1(1)
-    arrived(2)
-    mm1(2)
-    mm2(1)
-    mm2(2)
-    arrived(3)
-    mm1(3)
-    mm2(3)
+    for a, k in PIECES:
+        te.wait_ge(S["arr%d%d" % (a, order[k])], _bits(topo.mask(T.cores[order[k]], core)))
+        if a == 0:
+            mm1(k)
+        else:
+            mm2(k)
 
     ve.wait_ge(S.zs, 1)
     for k in range(N):

from concourse.mybir import AluOpType

N = 4
TK = 512
HALF = TK // 2
D = 128
STEPS = (1, 3, 2)
PIECES = ((0, 1), (0, 2), (1, 1), (0, 3), (1, 2), (1, 3))

SCRATCH = {
    "xs": ("sbuf", [128, TK], "bfloat16"),
    "zero": ("sbuf", [128, HALF], "float32"),
    "ys0": ("sbuf", [128, HALF], "bfloat16"),
    "ys1": ("sbuf", [128, HALF], "bfloat16"),
    "acc0": ("psum", [128, 512], "float32"),
    "acc1": ("psum", [128, 512], "float32"),
}
for _j in range(N):
    SCRATCH["wp%d" % _j] = ("sbuf", [128, 2 * D], "bfloat16")
    for _c in range(2):
        SCRATCH["h%d%d" % (_j, _c)] = ("sbuf", [128, HALF], "bfloat16")
for _b in range(6):
    SCRATCH["p%d" % _b] = ("psum", [128, 512], "float32")

SEMAPHORES = ["ldw1", "ldw2", "ldx", "zs", "sent", "st0", "st1", "m20", "m21", "cp0", "cp1"]
SEMAPHORES += ["arr%d%d" % (_a, _j) for _a in range(2) for _j in range(N)]
SEMAPHORES += ["m1%d%d" % (_k, _c) for _k in range(N) for _c in range(2)]
SEMAPHORES += ["rl%d%d" % (_k, _c) for _k in range(N) for _c in range(2)]


def _bits(mask):
    n = 0
    while mask:
        n += mask & 1
        mask >>= 1
    return n


def rank_program(g, core, T, topo):
    r = T.rank_of(core)
    if r is None:
        return
    te, ve, sy, sc = g.tensor, g.vector, g.sync, g.scalar
    S = T.sem
    own = T["wp%d" % r]

    sy.dma_start(own[0:64, 0:D], T.w1[0:64, :]).then_inc(S.ldw1, 16)
    sc.dma_start(own[64:128, 0:D], T.w1[64:128, :]).then_inc(S.ldw1, 16)
    sy.dma_start(own[:, D:2 * D], T.w2[:, :]).then_inc(S.ldw2, 16)
    sc.dma_start(T.xs[:, :], T.x[:, :]).then_inc(S.ldx, 16)
    ve.memset(T.zero[:, :], 0.0).then_inc(S.zs, 1)

    g.wait_ge(S.ldw1, 32)
    left = 0
    have_w2 = False
    for a, k in PIECES:
        if a == 1 and not have_w2:
            g.wait_ge(S.ldw2, 16)
            have_w2 = True
        dst = T.cores[(r + STEPS[k - 1]) % N]
        assert topo.may_write(core, dst)
        rid, pid, _ = topo.addr(dst)
        m = topo.mask(core, dst)
        ap = own[:, a * D:(a + 1) * D]
        g.remote_dma(ap, ap, S["arr%d%d" % (a, r)], S.sent, pid, rid, m)
        left += _bits(m)

    order = [r] + [(r - s) % N for s in STEPS]

    def mm1(k):
        w = T["wp%d" % order[k]]
        for c in range(2):
            te.matmul(T["p%d" % (2 * (k % 3) + c)][:, 0:HALF], w[:, 0:D], T.xs[:, c * HALF:(c + 1) * HALF],
                      True, True).then_inc(S["m1%d%d" % (k, c)], 1)

    def mm2(k):
        w = T["wp%d" % order[k]]
        for c in range(2):
            te.wait_ge(S["rl%d%d" % (k, c)], 1)
            i = te.matmul(T["acc%d" % c][:, 0:HALF], w[:, D:2 * D], T["h%d%d" % (k, c)][:, :], k == 0, k == N - 1)
            if k == N - 1:
                i.then_inc(S["m2%d" % c], 1)

    te.wait_ge(S.ldw1, 32)
    te.wait_ge(S.ldx, 16)
    mm1(0)
    te.wait_ge(S.ldw2, 16)
    mm2(0)
    for a, k in PIECES:
        te.wait_ge(S["arr%d%d" % (a, order[k])], _bits(topo.mask(T.cores[order[k]], core)))
        if a == 0:
            mm1(k)
        else:
            mm2(k)

    ve.wait_ge(S.zs, 1)
    for k in range(N):
        for c in range(2):
            ve.wait_ge(S["m1%d%d" % (k, c)], 1)
            ve.tensor_tensor(T["h%d%d" % (k, c)][:, :], T["p%d" % (2 * (k % 3) + c)][:, 0:HALF], T.zero[:, :],
                             AluOpType.max).then_inc(S["rl%d%d" % (k, c)], 1)
    for c in range(2):
        ve.wait_ge(S["m2%d" % c], 1)
        ve.tensor_copy(T["ys%d" % c][:, :], T["acc%d" % c][:, 0:HALF]).then_inc(S["cp%d" % c], 1)

    for c, q in ((0, sy), (1, sc)):
        q.wait_ge(S["cp%d" % c], 1)
        q.dma_start(T.y[:, c * HALF:(c + 1) * HALF], T["ys%d" % c][:, :]).then_inc(S["st%d" % c], 16)
        q.wait_ge(S["st%d" % c], 16)

    g.wait_ge(S.sent, left)
